import numpy as np, ml_dtypes
CORES = [83,85,87,115,117,119]
N = 6
import mx_ref
NC, ROOT = 128, 5
BF = ml_dtypes.bfloat16
def cut(t, i, w=512):
    return t[:, w * i:w * i + w]
def term(a, B):
    return np.stack([np.maximum(mx_ref.matmul(mx_ref.quantize(cut(a, i)), B), 0) for i in range(4)], axis=2).reshape(128, -1)
def setup_inputs(rng):
    def f(*shape):
        return mx_ref.flush((rng.standard_normal(shape, dtype=np.float32) * np.exp2(rng.integers(-2, 3, shape[:-1] + (1,)))).astype(BF))
    return {"a": f(N, 128, 4 * 512), "b": f(N, 128, 4 * NC)}
def setup_inputs_blocks(rng):
    d = setup_inputs(rng)
    for k in ("a", "b"): d[k] = mx_ref.spread(d[k], rng, 2)
    return d
def setup_inputs_wide(rng):
    d = setup_inputs(rng)
    for k in ("a", "b"): d[k] = mx_ref.flush((d[k].astype(np.float32) * np.exp2(rng.integers(-4, 5, (N, 1, 1))).astype(np.float32)).astype(BF))
    return d
def setup_inputs_lossless(rng):
    a = np.zeros((N, 128, 4 * 128, 4), np.float32)
    for r in range(N):
        k = rng.integers(0, 512, size=4 * 128)
        a[r, k // 4, np.arange(4 * 128), k % 4] = 1.0
    size = np.repeat(2.0 ** rng.integers(-4, 5, size=(1, 1, (4 * NC) // 4)), 4, axis=2)
    b = (rng.random((N, 128, 4 * NC)) < 0.8) * size
    return {"a": a.reshape(N, 128, 4 * 512).astype(BF), "b": b.astype(np.float32).astype(BF)}
def reference(a, b):
    B0 = mx_ref.quantize(b[ROOT])
    T = [term(a[r], B0) for r in range(N)]
    y = np.zeros((N, 128, 4 * NC), np.float32)
    y[:] = mx_ref.total(T)
    return {"y": y}

from concourse.bass import DstId, RemoteDMATransfer
from concourse.mybir import dt, AluOpType, ActivationFunctionType

X4 = "float8_e4m3fn_x4"
SCRATCH = {
    "bt": ("sbuf", [128, 512], "bfloat16"),
    "at": ("sbuf", [128, 2048], "bfloat16"),
    "jt": ("sbuf", [128, 512], "bfloat16"),
    "selt": ("sbuf", [128, 2048], "bfloat16"),
    "tt": ("sbuf", [128, 512], "bfloat16"),
    "pt": ("sbuf", [128, 512], "bfloat16"),
    "ds": ("sbuf", [128, 512], "float32"),
    "yt": ("sbuf", [128, 512], "float32"),
    "bq": ("sbuf", [128, 128], X4), "bs": ("sbuf", [128, 128], "uint8"),
    "aq": ("sbuf", [128, 512], X4), "as": ("sbuf", [128, 512], "uint8"),
    "selq": ("sbuf", [128, 512], X4), "sels": ("sbuf", [128, 512], "uint8"),
    "tq": ("sbuf", [128, 128], X4), "ts": ("sbuf", [128, 128], "uint8"),
    "lq": ("sbuf", [128, 128], X4), "ls": ("sbuf", [128, 128], "uint8"),
    "pq": ("sbuf", [128, 128], X4), "ps": ("sbuf", [128, 128], "uint8"),
    "g0q": ("sbuf", [128, 128], X4), "g0s": ("sbuf", [128, 128], "uint8"),
    "g1q": ("sbuf", [128, 128], X4), "g1s": ("sbuf", [128, 128], "uint8"),
    "wq": ("sbuf", [128, 128], X4), "ws": ("sbuf", [128, 128], "uint8"),
    "pp": ("psum", [128, 2048], "float32"),
    "dd": ("psum", [128, 2048], "float32"),
}
SEMAPHORES = (["ldb", "lda", "io", "selr", "qsel", "qb", "qa", "aB", "r", "qt", "aT", "u", "qp", "aP0", "aP1", "aW",
               "yc", "st", "loc", "dc"]
              + ["%s%d" % (s, b) for s in ("p", "s", "f", "e") for b in range(4)])
Relu, Copy = ActivationFunctionType.Relu, ActivationFunctionType.Copy


def engines(mask):
    return [1 << e for e in range(mask.bit_length()) if mask >> e & 1]


def roles(T, topo):
    cores = T.cores
    root = cores[T.root]
    home = [c for c in cores if topo.chip(c) == topo.chip(root)]
    away = [c for c in cores if topo.chip(c) != topo.chip(root)]
    near = [c for c in home if c != root]
    solo = [c for c in away if sum(topo.die(d) == topo.die(c) for d in away) == 1][0]
    direct = [c for c in away if c != solo]
    first = sorted(near, key=lambda c: topo.die(c) != topo.die(direct[0]))
    partner = {root: solo, solo: root}
    for d, n in zip(direct, first):
        partner[d] = n
        partner[n] = d
    return root, solo, near, direct, partner


def rank_program(g, core, T, topo):
    if T.rank_of(core) is None:
        return
    S = T.sem
    root, solo, near, direct, partner = roles(T, topo)
    is_root, is_solo, paired = core == root, core == solo, core in near or core in direct
    sent = [0]

    off_chip = topo.mask(root, solo)
    inside = topo.mask(root, near[0])
    rest = inside & ~off_chip

    def split(dsts, mask):
        e = engines(mask)
        order = sorted(dsts, key=lambda c: topo.die(c) == topo.die(core))
        return [([order[0]], sum(e[0::2])), ([order[1]], sum(e[1::2]))]

    def send(groups, names, sem, to=None):
        for k in range(2):
            tr = []
            for dsts, mask in groups:
                ids, outs = [], []
                for d in dsts:
                    rid, pnc, _ = topo.addr(d)
                    ids.append(DstId(rid=rid, pnc=pnc))
                    name = (to(d) if to else names)[k]
                    outs.append(T[name][:].bitcast(dt.uint8) if k == 0 else T[name][:])
                src = T[names[k]][:].bitcast(dt.uint8) if k == 0 else T[names[k]][:]
                sems = {sem(d) for d in dsts}
                tr.append(RemoteDMATransfer(dst_ids=ids, dma_engine_mask=mask, remote_sem=S[sems.pop()], srcs=[src], dsts=outs))
                sent[0] += len(engines(mask))
            g.remote_dma_fused(tr, local_sem=S["loc"])

    n_off, n_in, n_rest = len(engines(off_chip)), len(engines(inside)), len(engines(rest))

    if is_root:
        g.sync.dma_start(T.bt[:], T.b[:]).then_inc(S["ldb"], 16)
    g.sync.dma_start(T.at[:], T.a[:]).then_inc(S["lda"], 16)

    g.iota(T.jt[:], [[1, 512]], 0, -4, allow_small_or_imprecise_dtypes=True).then_inc(S["io"], 1)

    def selectors():
        g.vector.wait_ge(S["io"], 1)
        for b in range(4):
            g.vector.tensor_scalar(T.selt[:, 512 * b:512 * b + 512], T.jt[:], float(b), None, AluOpType.is_equal).then_inc(S["selr"], 1)
        g.vector.wait_ge(S["selr"], 4)
        g.vector.quantize_mx(T.selq[:], T.sels[:], T.selt[:]).then_inc(S["qsel"], 1)

    def bank(t, b):
        return t[:, 512 * b:512 * b + 128]

    def product(b, start=True):
        return g.tensor.matmul_mx(bank(T.pp, b), T.aq[:, 128 * b:128 * b + 128], T["as"][:, 128 * b:128 * b + 128],
                                  T.bq[:], T.bs[:], start, True)

    def add(t, b, names, start, stop):
        return g.tensor.matmul_mx(bank(t, b), T.selq[:, 128 * b:128 * b + 128], T.sels[:, 128 * b:128 * b + 128],
                                  T[names[0]][:], T[names[1]][:], start, stop)

    def drain(src, dst, ready, done, func):
        for b in (0, 2):
            g.scalar.wait_ge(S["%s%d" % (ready, b)], 1)
            g.scalar.activation(dst[:, b:512:4], bank(src, b), func).then_inc(S[done], 1)
        for b in (1, 3):
            g.vector.wait_ge(S["%s%d" % (ready, b)], 1)
            if func is Relu:
                g.vector.tensor_scalar(dst[:, b:512:4], bank(src, b), 0.0, None, AluOpType.max).then_inc(S[done], 1)
            else:
                g.vector.tensor_copy(dst[:, b:512:4], bank(src, b)).then_inc(S[done], 1)

    if is_root:
        g.vector.wait_ge(S["ldb"], 16)
        g.vector.quantize_mx(T.bq[:], T.bs[:], T.bt[:]).then_inc(S["qb"], 1)
    else:
        selectors()
    g.vector.wait_ge(S["lda"], 16)
    g.vector.quantize_mx(T.aq[:], T["as"][:], T.at[:]).then_inc(S["qa"], 1)

    b_name, b_count = ("qb", 1) if is_root else ("aB", 2 * (n_off if core in direct else n_rest // 2 if core in near else n_in))
    if is_root:
        g.wait_ge(S["qb"], 1)
        send([([direct[0]], off_chip)], ("bq", "bs"), lambda d: "aB")
        send([([direct[1]], off_chip)] + split(near, rest), ("bq", "bs"), lambda d: "aB")
    elif core == direct[0]:
        g.wait_ge(S["aB"], b_count)
        send([([solo], inside)], ("bq", "bs"), lambda d: "aB")

    g.tensor.wait_ge(S["qa"], 1)
    if is_solo:
        g.tensor.wait_ge(S["qsel"], 1)
        g.tensor.wait_ge(S["aT"], 2 * n_off)
        for b in range(4):
            add(T.dd, b, ("lq", "ls"), True, True).then_inc(S["e%d" % b], 1)
        for b in range(4):
            add(T.pp, b, ("lq", "ls"), True, False)
        g.tensor.wait_ge(S[b_name], b_count)
        for b in range(4):
            product(b, False).then_inc(S["p%d" % b], 1)
        for b in range(4):
            g.scalar.wait_ge(S["e%d" % b], 1)
            g.scalar.activation(T.ds[:, 128 * b:128 * b + 128], bank(T.dd, b), Copy).then_inc(S["dc"], 1)
        g.vector.wait_ge(S["dc"], 4)
        for b in range(4):
            g.vector.wait_ge(S["p%d" % b], 1)
            g.vector.tensor_tensor(T.pt[:, b:512:4], bank(T.pp, b), T.ds[:, 128 * b:128 * b + 128], AluOpType.max).then_inc(S["u"], 1)
        g.vector.wait_ge(S["u"], 4)
        g.vector.quantize_mx(T.wq[:], T.ws[:], T.pt[:]).then_inc(S["qp"], 1)
        g.wait_ge(S["qp"], 1)
        send([([root] + near, off_chip)], ("wq", "ws"), lambda d: "aW")
        send(split(direct, rest), ("wq", "ws"), lambda d: "aW")
    else:
        g.tensor.wait_ge(S[b_name], b_count)
        for b in range(4):
            product(b).then_inc(S["p%d" % b], 1)
        drain(T.pp, T.tt, "p", "r", Relu)
        g.vector.wait_ge(S["r"], 4)
        g.vector.quantize_mx(T.tq[:], T.ts[:], T.tt[:]).then_inc(S["qt"], 1)
        g.wait_ge(S["qt"], 1)
        send([([partner[core]], off_chip)], ("tq", "ts"), lambda d: "aT", lambda d: ("lq", "ls"))
        if is_root:
            selectors()

    if paired:
        mates = near if core in near else direct
        hub = root if core in near else solo
        g.tensor.wait_ge(S["qsel"], 1)
        g.tensor.wait_ge(S["qt"], 1)
        for b in range(4):
            add(T.dd, b, ("tq", "ts"), True, False)
        for b in range(4):
            add(T.pp, b, ("tq", "ts"), True, False)
        g.tensor.wait_ge(S["aT"], 2 * n_off)
        for b in range(4):
            add(T.dd, b, ("lq", "ls"), False, True).then_inc(S["s%d" % b], 1)
        for b in range(4):
            add(T.pp, b, ("lq", "ls"), False, False)
        drain(T.dd, T.pt, "s", "u", Copy)
        g.vector.wait_ge(S["u"], 4)
        g.vector.quantize_mx(T.pq[:], T.ps[:], T.pt[:]).then_inc(S["qp"], 1)
        g.wait_ge(S["qp"], 1)
        slot = mates.index(core)
        other = mates[1 - slot]
        send(split([other, hub], inside), ("pq", "ps"),
             lambda d: "aP%d" % (slot if d == hub else 0),
             lambda d: ("g%dq" % (slot if d == hub else 0), "g%ds" % (slot if d == hub else 0)))

    acc = T.dd if is_root else T.pp
    if is_root:
        g.tensor.wait_ge(S["qsel"], 1)
    if is_solo:
        g.tensor.wait_ge(S["qp"], 1)
    steps = [("g0q", "g0s", "aP0", n_in), ("g1q", "g1s", "aP1", n_in), ("wq", "ws", "aW", 2 * n_off if is_root or core in near else n_rest)]
    if is_solo:
        steps = [("wq", "ws", None, 0)] + steps[:2]
    elif paired:
        steps = [steps[0], steps[2]]
    for k, (q, s, sem, n) in enumerate(steps):
        if sem:
            g.tensor.wait_ge(S[sem], n)
        last = k == len(steps) - 1
        for b in range(4):
            m = add(acc, b, (q, s), k == 0 and not paired, last)
            if last:
                m.then_inc(S["f%d" % b], 1)
    drain(acc, T.yt, "f", "yc", Copy)
    g.sync.wait_ge(S["yc"], 4)
    g.sync.dma_start(T.y[:], T.yt[:]).then_inc(S["st"], 16)
    g.sync.wait_ge(S["st"], 16)
    if sent[0]:
        g.wait_ge(S["loc"], sent[0])
